import numpy as np
import ml_dtypes


def mxq(x, axis, fmt="e4m3"):
    dtype, down = {"e4m3": (ml_dtypes.float8_e4m3fn, 7), "e5m2": (ml_dtypes.float8_e5m2, 14)}[fmt]
    v = np.moveaxis(np.asarray(x, np.float32).astype(ml_dtypes.bfloat16).astype(np.float64), axis, -1)
    blocks = v.reshape(v.shape[:-1] + (-1, 32))
    amax = np.abs(blocks).max(-1, keepdims=True)
    byte = np.maximum(np.where(amax > 0, np.frexp(amax)[1] - 1 + 127, 0) - down, 1)
    scale = np.exp2(byte - 127.0)
    codes = (blocks / scale).astype(np.float32).astype(dtype).astype(np.float64)
    return np.moveaxis((codes * scale).reshape(v.shape), -1, axis)


WIDE = False


def mx_kscale(k):
    if not WIDE:
        return np.ones(k)
    levels = np.array([18, -18])
    if k % 512:
        return np.exp2(np.random.permutation(np.resize(levels, k // 32))).repeat(32)
    a = np.empty((k // 512, 16))
    for p in range(k // 512):
        a[p, :8] = np.random.permutation(np.resize(levels, 8))
        for g in range(8):
            far = levels[np.abs(levels - a[p, g]) >= 10]
            a[p, g + 8] = far[np.random.randint(len(far))]
    return np.exp2(a.ravel()).repeat(32)


def f64(x):
    return np.asarray(x).astype(np.float64)


def striped(idx):
    return np.tile(np.asarray(idx).reshape(-1, 16).T, (8, 1)).astype(np.uint16)


def unstriped(offs):
    return offs[:16].T.reshape(-1).astype(np.int64)


def setup_inputs():
    n = np.random.standard_normal
    uni = np.random.uniform
    idx = np.random.permutation(2048)[:512]
    f_d = mx_kscale(512)
    f_r = mx_kscale(512)
    return {
        "xT": (0.5 * n((512, 512)) * f_d[:, None] * f_r[None, :]).astype(np.float32),
        "wl": (n((512, 2048)) / np.sqrt(512) / f_d[:, None]).astype(np.float32),
        "wm": (n((512, 2048)) / np.sqrt(512) / f_d[:, None]).astype(np.float32),
        "y": (n((512, 1))).astype(np.float32),
        "us": (uni(0.75, 1.3, (512, 1)) / f_r[:, None]).astype(np.float32),
        "tl": np.tile(uni(0.75, 1.3, 2048), (128, 1)).astype(np.float32),
        "tm": np.tile(uni(0.75, 1.3, 2048), (128, 1)).astype(np.float32),
        "wt": (uni(0.75, 1.3, (512, 1))).astype(np.float32),
        "offs": striped(idx),
    }


def reference(xT, wl, wm, y, us, tl, tm, wt, offs):
    idx = unstriped(offs)
    wl_i = f64(wl)[:, idx]
    wm_i = f64(wm)[:, idx]
    tl_i = f64(tl)[:1][:, idx]
    tm_i = f64(tm)[:1][:, idx]
    q_xT = mxq(f64(xT), 0, "e4m3")
    a = q_xT.T @ mxq(wl_i, 0, "e4m3")
    b = q_xT.T @ mxq(wm_i, 0, "e4m3")
    l = f64(us) * tl_i * a
    q = f64(us) * tm_i * b - f64(y)
    m = (l).max(-1, keepdims=True)
    e = np.exp(l - m)
    te = (e).sum(-1, keepdims=True)
    s = l - 0.5 * np.square(q)
    ms = (s).max(-1, keepdims=True)
    f = np.exp(s - ms)
    tf = (f).sum(-1, keepdims=True)
    po = f / tf
    gl = f64(wt) * f64(us) * tl_i * (e / te - po)
    gm = f64(wt) * f64(us) * tm_i * po * q
    q_xT_2 = mxq(f64(xT), 1, "e4m3")
    d1 = q_xT_2 @ mxq(gl, 0, "e5m2")
    d2 = q_xT_2 @ mxq(gm, 0, "e5m2")
    out_0 = np.zeros((512, 2048))
    out_0[:, idx] = d1
    out_1 = np.zeros((512, 2048))
    out_1[:, idx] = d2
    return out_0, out_1

@@ -1,0 +1,251 @@
+from contextlib import ExitStack
+
+import concourse.mybir as mybir
+from concourse.masks import make_identity
+
+F32 = mybir.dt.float32
+BF16 = mybir.dt.bfloat16
+U32 = mybir.dt.uint32
+U16 = mybir.dt.uint16
+U8 = mybir.dt.uint8
+E4M3 = mybir.dt.float8_e4m3fn_x4
+E5M2 = mybir.dt.float8_e5m2_x4
+ALU = mybir.AluOpType
+ACT = mybir.ActivationFunctionType
+AXIS = mybir.AxisListType
+
+P = 128
+PACK = 4
+D = 512
+R = 512
+SLOTS = 512
+COLS = 2048
+WINDOWS = 3
+
+FLOPS = 4 * 2 * D * R * SLOTS
+
+
+def tile_attend_gmdn_w_kernel(tc, xT, wl, wm, y, us, tl, tm, wt, offs, out_0, out_1):
+    nc = tc.nc
+    with ExitStack() as ctx:
+        keep = ctx.enter_context(tc.tile_pool(name="keep", bufs=1))
+        stage = ctx.enter_context(tc.tile_pool(name="stage", bufs=4))
+        psum_a = ctx.enter_context(tc.psum_pool(name="psum_a", bufs=4))
+        psum_b = ctx.enter_context(tc.psum_pool(name="psum_b", bufs=4))
+
+        def bank_a(name):
+            return psum_a.tile([P, PACK, P], F32, name=name, tag="a")
+
+        def bank_b(name):
+            return psum_b.tile([P, PACK, P], F32, name=name, tag="b")
+
+        def flat(t):
+            return t[:].rearrange("p a b -> p (a b)")
+
+        def quantise(name, src, fmt, tag=None):
+            codes = keep.tile([P, SLOTS], U32, name=name + "_codes", tag=tag or name + "_codes", align_bytes=64)
+            scales = keep.tile([P, SLOTS], U8, name=name + "_scales", tag=name + "_scales", align_bytes=64)
+            nc.vector.quantize_mx(out=codes[:].bitcast(fmt), scales=scales[:], in_=src)
+            return codes, scales
+
+        def product(acc, stat, stat_fmt, j, mov, mov_fmt):
+            cols = slice(j * P, (j + 1) * P)
+            nc.tensor.matmul_mx(
+                out=flat(acc), lhsT=stat[0][:, cols].bitcast(stat_fmt), lhsT_scale=stat[1][:, cols],
+                rhs=mov[0][:].bitcast(mov_fmt), rhs_scale=mov[1][:], start=True, stop=True)
+
+        offsets = keep.tile([P, SLOTS // 16], U16, name="offsets")
+        nc.sync.dma_start(offsets[:], offs)
+        y_sb = keep.tile([P, PACK], F32, name="y_sb")
+        us_sb = keep.tile([P, PACK], F32, name="us_sb")
+        wt_sb = keep.tile([P, PACK], F32, name="wt_sb")
+        for dst, src in ((us_sb, us), (wt_sb, wt), (y_sb, y)):
+            nc.scalar.dma_start(out=dst[:], in_=src.rearrange("(s t) o -> s (t o)", t=PACK))
+
+        x_raw = keep.tile([P, PACK, R], F32, name="x_raw")
+        nc.sync.dma_start(out=x_raw[:], in_=xT.rearrange("(p j) r -> p j r", j=PACK))
+
+        tl_win = keep.tile([P, COLS], F32, name="tl_win")
+        tm_win = keep.tile([P, COLS], F32, name="tm_win")
+        nc.vector.memset(tl_win[:], 0.0)
+        nc.vector.memset(tm_win[:], 0.0)
+
+        planes = {}
+        for name, table in (("wl", wl), ("wm", wm)):
+            rows = table.rearrange("(p j) c -> j p c", j=PACK)
+            for j in range(PACK):
+                plane = keep.tile([P, COLS], F32, name="%s_plane%d" % (name, j))
+                nc.sync.dma_start(out=plane[:], in_=rows[j])
+                planes[name, j] = plane
+                if name == "wl" and j == 0:
+                    nc.sync.dma_start(out=tl_win[0:1, :], in_=tl[0:1, :])
+                if name == "wl" and j == 1:
+                    nc.sync.dma_start(out=tm_win[0:1, :], in_=tm[0:1, :])
+
+        ident = keep.tile([P, P], F32, name="ident")
+        make_identity(nc, ident[:])
+
+        warm = keep.tile([P, 2], F32, name="warm")
+        nc.scalar.activation(warm[:], ident[:, 0:2], ACT.Exp)
+
+        neg_us = keep.tile([P, PACK], F32, name="neg_us")
+        neg_y = keep.tile([P, PACK], F32, name="neg_y")
+        wu = keep.tile([P, PACK], F32, name="wu")
+        neg_wu = keep.tile([P, PACK], F32, name="neg_wu")
+        neg_wuy = keep.tile([P, PACK], F32, name="neg_wuy")
+        nc.gpsimd.tensor_scalar(neg_us[:], us_sb[:], -1.0, 0.0, ALU.mult, ALU.add)
+        nc.gpsimd.tensor_scalar(neg_y[:], y_sb[:], -1.0, 0.0, ALU.mult, ALU.add)
+        nc.gpsimd.tensor_tensor(wu[:], wt_sb[:], us_sb[:], ALU.mult)
+        nc.gpsimd.tensor_tensor(neg_wu[:], wt_sb[:], neg_us[:], ALU.mult)
+        nc.gpsimd.tensor_tensor(neg_wuy[:], wu[:], neg_y[:], ALU.mult)
+
+        x_d = keep.tile([P, PACK, P, PACK], BF16, name="x_d", align_bytes=64)
+        nc.scalar.copy(x_d[:], x_raw[:].rearrange("p j (s t) -> p t s j", t=PACK))
+
+        x_r = keep.tile([P, PACK, P, PACK], BF16, name="x_r", align_bytes=64)
+        for j in range(PACK):
+            turned = bank_a("x_turned%d" % j)
+            for t in range(PACK):
+                nc.tensor.transpose(turned[:, t, :], x_raw[:, j, t::PACK], ident[:])
+            nc.scalar.copy(x_r[:, j, :, :], turned[:].rearrange("s t p -> s p t"))
+
+        cols = {}
+        spread = {}
+        for name, win in (("tl", tl_win), ("tm", tm_win)):
+            picked = keep.tile([P, SLOTS], F32, name=name + "_picked")
+            nc.vector.tensor_copy(picked[:], win[:].indirect(offsets[:]))
+            turned = bank_b(name + "_turned")
+            for k in range(PACK):
+                nc.tensor.transpose(turned[:, k, :], picked[:, k * P:(k + 1) * P], ident[:])
+            col = keep.tile([P, PACK], F32, name=name + "_col")
+            nc.scalar.copy(col[:], turned[:, :, 0])
+            cols[name] = col
+            row = bank_b(name + "_row")
+            for k in range(PACK):
+                nc.tensor.transpose(row[:, k, :], col[:, k:k + 1].to_broadcast([P, P]), ident[:])
+            spread[name] = row
+        tm_row = keep.tile([P, SLOTS], F32, name="tm_row")
+        nc.scalar.copy(tm_row[:], flat(spread["tm"]))
+        tl_wu = keep.tile([P, PACK, SLOTS], F32, name="tl_wu")
+        for t in range(PACK):
+            nc.scalar.activation(tl_wu[:, t, :], flat(spread["tl"]), ACT.Copy, scale=neg_wu[:, t:t + 1])
+
+        wl_i = keep.tile([P, SLOTS, PACK], BF16, name="wl_i", align_bytes=64)
+        for j in range(2):
+            nc.vector.tensor_copy(wl_i[:, :, j], planes["wl", j][:].indirect(offsets[:]))
+        xq_d = quantise("x_d", x_d[:].rearrange("p t s j -> p (t s j)"), E4M3)
+        nc.vector.tensor_copy(wl_i[:, :, 2], planes["wl", 2][:].indirect(offsets[:]))
+        nc.vector.tensor_copy(wl_i[:, :, 3], planes["wl", 3][:].indirect(offsets[:]))
+        wlq = quantise("wl", flat(wl_i), E4M3)
+
+        wm_i = keep.tile([P, SLOTS, PACK], BF16, name="wm_i", tag="wm_i", align_bytes=64)
+        wm_pair = keep.tile([P, 2, SLOTS], F32, name="wm_pair")
+        nc.vector.tensor_copy(wm_pair[:, 0, :], planes["wm", 0][:].indirect(offsets[:]))
+
+        a_tl = keep.tile([P, PACK, R], F32, name="a_tl", tag="a_tl")
+        for k in range(PACK):
+            acc = bank_a("a%d" % k)
+            product(acc, wlq, E4M3, k, xq_d, E4M3)
+            nc.scalar.activation(a_tl[:, k, :], flat(acc), ACT.Copy, scale=cols["tl"][:, k:k + 1])
+
+        nc.vector.tensor_copy(wm_pair[:, 1, :], planes["wm", 1][:].indirect(offsets[:]))
+        nc.scalar.copy(wm_i[:, :, 0:2], wm_pair[:].rearrange("p j i -> p i j"))
+
+        neg_l = keep.tile([P, PACK, SLOTS], F32, name="neg_l")
+        neg_m = keep.tile([P, PACK], F32, name="neg_m")
+        te = keep.tile([P, PACK], F32, name="te")
+        e = keep.tile([P, PACK, SLOTS], F32, name="e")
+        for t in range(PACK):
+            back = bank_b("l_back%d" % t)
+            for k in range(PACK):
+                nc.tensor.transpose(back[:, k, :], a_tl[:, k, t * P:(t + 1) * P], ident[:])
+            nc.vector.tensor_scalar(neg_l[:, t, :], flat(back), neg_us[:, t:t + 1], None, ALU.mult, ALU.min,
+                                    accum_out=neg_m[:, t:t + 1])
+            nc.scalar.activation(e[:, t, :], neg_l[:, t, :], ACT.Exp, bias=neg_m[:, t:t + 1], scale=-1.0,
+                                 accum_out=te[:, t:t + 1])
+            if t == 1:
+                nc.vector.tensor_copy(wm_i[:, :, 2], planes["wm", 2][:].indirect(offsets[:]))
+        nc.vector.tensor_copy(wm_i[:, :, 3], planes["wm", 3][:].indirect(offsets[:]))
+        wmq = quantise("wm", flat(wm_i), E4M3)
+        xq_r = quantise("x_r", x_r[:].rearrange("s j p t -> s (j p t)"), E4M3, tag="wm_i")
+        inv_te = keep.tile([P, PACK], F32, name="inv_te")
+        nc.vector.reciprocal(inv_te[:], te[:])
+
+        mean = keep.tile([P, PACK, SLOTS], F32, name="mean")
+        neg_s = keep.tile([P, PACK, SLOTS], F32, name="neg_s", tag="neg_s")
+        for t in range(PACK):
+            acc = bank_a("b%d" % t)
+            product(acc, xq_d, E4M3, t, wmq, E4M3)
+            nc.vector.scalar_tensor_tensor(mean[:, t, :], flat(acc), us_sb[:, t:t + 1], tm_row[:], ALU.mult, ALU.mult)
+            nc.scalar.activation(neg_s[:, t, :], mean[:, t, :], ACT.Square, bias=neg_y[:, t:t + 1])
+
+        windows = []
+        for tag in ("x_d_scales", "wm_codes", "wm_scales"):
+            window = keep.tile([P, COLS], F32, name="window_" + tag, tag=tag, align_bytes=64)
+            nc.gpsimd.memset(window[:], 0.0)
+            windows.append(window)
+
+        neg_ms = keep.tile([P, PACK], F32, name="neg_ms")
+        tf = keep.tile([P, PACK], F32, name="tf")
+        inv_tf = keep.tile([P, PACK], F32, name="inv_tf")
+        f = keep.tile([P, PACK, SLOTS], F32, name="f", tag="a_tl")
+        for pair in ((0, 1), (2, 3)):
+            for t in pair:
+                nc.vector.scalar_tensor_tensor(neg_s[:, t, :], neg_s[:, t, :], 0.5, neg_l[:, t, :], ALU.mult, ALU.add)
+            for t in pair:
+                nc.vector.tensor_reduce(neg_ms[:, t:t + 1], neg_s[:, t, :], AXIS.X, ALU.min)
+                nc.scalar.activation(f[:, t, :], neg_s[:, t, :], ACT.Exp, bias=neg_ms[:, t:t + 1], scale=-1.0,
+                                     accum_out=tf[:, t:t + 1])
+                nc.scalar.activation(e[:, t, :], e[:, t, :], ACT.Copy, scale=inv_te[:, t:t + 1])
+        for pair in ((0, 1), (2, 3)):
+            both = slice(pair[0], pair[1] + 1)
+            nc.vector.reciprocal(inv_tf[:, both], tf[:, both])
+            for t in pair:
+                nc.vector.scalar_tensor_tensor(e[:, t, :], f[:, t, :], inv_tf[:, t:t + 1], e[:, t, :],
+                                               ALU.mult, ALU.subtract)
+        gl = keep.tile([P, SLOTS, PACK], BF16, name="gl", tag="gl", align_bytes=64)
+        nc.vector.tensor_tensor(gl[:].rearrange("p (c i) t -> p c t i", i=2),
+                                e[:].rearrange("p t (c i) -> p c t i", i=2),
+                                tl_wu[:].rearrange("p t (c i) -> p c t i", i=2), ALU.mult)
+        glq = quantise("gl", flat(gl), E5M2)
+        q_wu = keep.tile([P, PACK, SLOTS], F32, name="q_wu", tag="neg_s")
+        po_q = keep.tile([P, PACK, SLOTS], F32, name="po_q", tag="gl", align_bytes=64)
+        for t in range(PACK):
+            nc.scalar.activation(q_wu[:, t, :], mean[:, t, :], ACT.Identity, bias=neg_wuy[:, t:t + 1],
+                                 scale=wu[:, t:t + 1])
+        for t in range(PACK):
+            nc.vector.scalar_tensor_tensor(po_q[:, t, :], f[:, t, :], inv_tf[:, t:t + 1], q_wu[:, t, :],
+                                           ALU.mult, ALU.mult)
+
+        def gradient_tile(n, grad, acc, j, out):
+            product(acc, xq_r, E4M3, j, grad, E5M2)
+            staged = stage.tile([P, SLOTS], F32, name="staged")
+            nc.scalar.copy(staged[:], flat(acc))
+            window = windows[n % WINDOWS]
+            nc.vector.tensor_copy(window[:].indirect(offsets[:]), staged[:])
+            nc.sync.dma_start(out=out.rearrange("(p j) c -> j p c", j=PACK)[j], in_=window[:])
+
+        for j in range(2):
+            gradient_tile(j, glq, bank_a("d1_%d" % j), j, out_0)
+
+        gm_t = keep.tile([P, PACK, 2, P, 2], BF16, name="gm_t")
+        for k in range(PACK):
+            turned = bank_b("gm_turned%d" % k)
+            for t in range(PACK):
+                nc.tensor.transpose(turned[:, t, :], po_q[:, t, k * P:(k + 1) * P], ident[:])
+            nc.scalar.activation(gm_t[:, k, :, :, :], turned[:].rearrange("n (u h) s -> n u s h", h=2), ACT.Copy,
+                                 scale=cols["tm"][:, k:k + 1])
+        for j in range(2, PACK):
+            gradient_tile(j, glq, bank_a("d1_%d" % j), j, out_0)
+        gm_words = gm_t[:].rearrange("n k u s h -> n (k u s h)").bitcast(F32)
+        gm = keep.tile([P, SLOTS, PACK], BF16, name="gm", align_bytes=64)
+        gm_pairs = flat(gm).bitcast(F32).rearrange("s (k n u) -> s k n u", k=PACK, u=2)
+        for half in range(2):
+            back = bank_b("gm_back%d" % half)
+            for c in range(PACK):
+                w0 = (PACK * half + c) * P
+                nc.tensor.transpose(back[:, c, :], gm_words[:, w0:w0 + P], ident[:])
+            nc.scalar.copy(gm_pairs[:, 2 * half:2 * half + 2, :, :], back[:].rearrange("s (k u) n -> s k n u", u=2))
+        gmq = quantise("gm", flat(gm), E5M2)
+        for j in range(PACK):
+            gradient_tile(PACK + j, gmq, bank_b("d2_%d" % j), j, out_1)

@@ -62,25 +62,25 @@ def tile_attend_gmdn_w_kernel(tc, xT, wl, wm, y, us, tl, tm, wt, offs, out_0, ou
         for dst, src in ((us_sb, us), (wt_sb, wt), (y_sb, y)):
             nc.scalar.dma_start(out=dst[:], in_=src.rearrange("(s t) o -> s (t o)", t=PACK))
 
-        x_raw = keep.tile([P, PACK, R], F32, name="x_raw")
-        nc.sync.dma_start(out=x_raw[:], in_=xT.rearrange("(p j) r -> p j r", j=PACK))
 
-        tl_win = keep.tile([P, COLS], F32, name="tl_win")
+        tl_win = keep.tile([P, COLS], F32, name="tl_win", tag="tl_win", align_bytes=64)
         tm_win = keep.tile([P, COLS], F32, name="tm_win")
         nc.vector.memset(tl_win[:], 0.0)
         nc.vector.memset(tm_win[:], 0.0)
+        x_raw = keep.tile([P, PACK, R], F32, name="x_raw")
+
+        nc.scalar.dma_start(out=tl_win[0:1, :], in_=tl[0:1, :])
+        nc.scalar.dma_start(out=tm_win[0:1, :], in_=tm[0:1, :])
+        nc.sync.dma_start(out=x_raw[:], in_=xT.rearrange("(p j) r -> p j r", j=PACK))
 
         planes = {}
         for name, table in (("wl", wl), ("wm", wm)):
             rows = table.rearrange("(p j) c -> j p c", j=PACK)
             for j in range(PACK):
-                plane = keep.tile([P, COLS], F32, name="%s_plane%d" % (name, j))
+                plane = keep.tile([P, COLS], F32, name="%s_plane%d" % (name, j), tag="%s_plane%d" % (name, j),
+                                  align_bytes=64)
                 nc.sync.dma_start(out=plane[:], in_=rows[j])
                 planes[name, j] = plane
-                if name == "wl" and j == 0:
-                    nc.sync.dma_start(out=tl_win[0:1, :], in_=tl[0:1, :])
-                if name == "wl" and j == 1:
-                    nc.sync.dma_start(out=tm_win[0:1, :], in_=tm[0:1, :])
 
         ident = keep.tile([P, P], F32, name="ident")
         make_identity(nc, ident[:])
@@ -103,73 +103,78 @@ def tile_attend_gmdn_w_kernel(tc, xT, wl, wm, y, us, tl, tm, wt, offs, out_0, ou
         nc.scalar.copy(x_d[:], x_raw[:].rearrange("p j (s t) -> p t s j", t=PACK))
 
         x_r = keep.tile([P, PACK, P, PACK], BF16, name="x_r", align_bytes=64)
-        for j in range(PACK):
+
+        def turn_x(j):
             turned = bank_a("x_turned%d" % j)
             for t in range(PACK):
                 nc.tensor.transpose(turned[:, t, :], x_raw[:, j, t::PACK], ident[:])
             nc.scalar.copy(x_r[:, j, :, :], turned[:].rearrange("s t p -> s p t"))
 
-        cols = {}
-        spread = {}
-        for name, win in (("tl", tl_win), ("tm", tm_win)):
-            picked = keep.tile([P, SLOTS], F32, name=name + "_picked")
+        def slot_scales(name, win, tag):
+            picked = keep.tile([P, SLOTS], F32, name=name + "_picked", tag=tag, align_bytes=64)
             nc.vector.tensor_copy(picked[:], win[:].indirect(offsets[:]))
             turned = bank_b(name + "_turned")
             for k in range(PACK):
                 nc.tensor.transpose(turned[:, k, :], picked[:, k * P:(k + 1) * P], ident[:])
             col = keep.tile([P, PACK], F32, name=name + "_col")
             nc.scalar.copy(col[:], turned[:, :, 0])
-            cols[name] = col
             row = bank_b(name + "_row")
             for k in range(PACK):
                 nc.tensor.transpose(row[:, k, :], col[:, k:k + 1].to_broadcast([P, P]), ident[:])
-            spread[name] = row
+            return col, row
+
+        def gather(dst, name, j):
+            nc.vector.tensor_copy(dst, planes[name, j][:].indirect(offsets[:]))
+
+        wl_i = keep.tile([P, SLOTS, PACK], BF16, name="wl_i", tag="wl_i", align_bytes=64)
+        for j in range(PACK):
+            turn_x(j)
+        tl_col, tl_spread = slot_scales("tl", tl_win, "tl_picked")
+        tm_col, tm_spread = slot_scales("tm", tm_win, "tl_win")
+        gather(wl_i[:, :, 0], "wl", 0)
+        gather(wl_i[:, :, 1], "wl", 1)
+        tl_row = keep.tile([P, SLOTS], F32, name="tl_row")
+        nc.scalar.copy(tl_row[:], flat(tl_spread))
         tm_row = keep.tile([P, SLOTS], F32, name="tm_row")
-        nc.scalar.copy(tm_row[:], flat(spread["tm"]))
+        nc.scalar.copy(tm_row[:], flat(tm_spread))
         tl_wu = keep.tile([P, PACK, SLOTS], F32, name="tl_wu")
         for t in range(PACK):
-            nc.scalar.activation(tl_wu[:, t, :], flat(spread["tl"]), ACT.Copy, scale=neg_wu[:, t:t + 1])
-
-        wl_i = keep.tile([P, SLOTS, PACK], BF16, name="wl_i", align_bytes=64)
-        for j in range(2):
-            nc.vector.tensor_copy(wl_i[:, :, j], planes["wl", j][:].indirect(offsets[:]))
+            nc.scalar.activation(tl_wu[:, t, :], flat(tl_spread), ACT.Copy, scale=neg_wu[:, t:t + 1])
         xq_d = quantise("x_d", x_d[:].rearrange("p t s j -> p (t s j)"), E4M3)
-        nc.vector.tensor_copy(wl_i[:, :, 2], planes["wl", 2][:].indirect(offsets[:]))
-        nc.vector.tensor_copy(wl_i[:, :, 3], planes["wl", 3][:].indirect(offsets[:]))
+        gather(wl_i[:, :, 2], "wl", 2)
+        gather(wl_i[:, :, 3], "wl", 3)
         wlq = quantise("wl", flat(wl_i), E4M3)
 
+        wm_pair = keep.tile([P, 2, SLOTS], F32, name="wm_pair", tag="wl_i", align_bytes=64)
         wm_i = keep.tile([P, SLOTS, PACK], BF16, name="wm_i", tag="wm_i", align_bytes=64)
-        wm_pair = keep.tile([P, 2, SLOTS], F32, name="wm_pair")
-        nc.vector.tensor_copy(wm_pair[:, 0, :], planes["wm", 0][:].indirect(offsets[:]))
-
-        a_tl = keep.tile([P, PACK, R], F32, name="a_tl", tag="a_tl")
-        for k in range(PACK):
-            acc = bank_a("a%d" % k)
-            product(acc, wlq, E4M3, k, xq_d, E4M3)
-            nc.scalar.activation(a_tl[:, k, :], flat(acc), ACT.Copy, scale=cols["tl"][:, k:k + 1])
-
-        nc.vector.tensor_copy(wm_pair[:, 1, :], planes["wm", 1][:].indirect(offsets[:]))
-        nc.scalar.copy(wm_i[:, :, 0:2], wm_pair[:].rearrange("p j i -> p i j"))
-
-        neg_l = keep.tile([P, PACK, SLOTS], F32, name="neg_l")
-        neg_m = keep.tile([P, PACK], F32, name="neg_m")
         te = keep.tile([P, PACK], F32, name="te")
         e = keep.tile([P, PACK, SLOTS], F32, name="e")
-        for t in range(PACK):
-            back = bank_b("l_back%d" % t)
-            for k in range(PACK):
-                nc.tensor.transpose(back[:, k, :], a_tl[:, k, t * P:(t + 1) * P], ident[:])
-            nc.vector.tensor_scalar(neg_l[:, t, :], flat(back), neg_us[:, t:t + 1], None, ALU.mult, ALU.min,
-                                    accum_out=neg_m[:, t:t + 1])
+
+        def log_weights(t, neg_l):
+            acc = bank_a("a%d" % t)
+            product(acc, xq_d, E4M3, t, wlq, E4M3)
+            nc.vector.scalar_tensor_tensor(neg_l[:, t, :], flat(acc), neg_us[:, t:t + 1], tl_row[:],
+                                           ALU.mult, ALU.mult)
+
+        def weights(t, neg_l, neg_m):
+            nc.vector.tensor_reduce(neg_m[:, t:t + 1], neg_l[:, t, :], AXIS.X, ALU.min)
             nc.scalar.activation(e[:, t, :], neg_l[:, t, :], ACT.Exp, bias=neg_m[:, t:t + 1], scale=-1.0,
                                  accum_out=te[:, t:t + 1])
-            if t == 1:
-                nc.vector.tensor_copy(wm_i[:, :, 2], planes["wm", 2][:].indirect(offsets[:]))
-        nc.vector.tensor_copy(wm_i[:, :, 3], planes["wm", 3][:].indirect(offsets[:]))
+
+        gather(wm_pair[:, 0, :], "wm", 0)
+        neg_l = keep.tile([P, PACK, SLOTS], F32, name="neg_l", tag="wm_plane0", align_bytes=64)
+        for t in range(PACK):
+            log_weights(t, neg_l)
+        gather(wm_pair[:, 1, :], "wm", 1)
+        nc.scalar.copy(wm_i[:, :, 0:2], wm_pair[:].rearrange("p j i -> p i j"))
+        neg_m = keep.tile([P, PACK], F32, name="neg_m", tag="wm_plane1", align_bytes=64)
+        for t in range(PACK):
+            weights(t, neg_l, neg_m)
+        gather(wm_i[:, :, 2], "wm", 2)
+        gather(wm_i[:, :, 3], "wm", 3)
         wmq = quantise("wm", flat(wm_i), E4M3)
         xq_r = quantise("x_r", x_r[:].rearrange("s j p t -> s (j p t)"), E4M3, tag="wm_i")
         inv_te = keep.tile([P, PACK], F32, name="inv_te")
-        nc.vector.reciprocal(inv_te[:], te[:])
 
         mean = keep.tile([P, PACK, SLOTS], F32, name="mean")
         neg_s = keep.tile([P, PACK, SLOTS], F32, name="neg_s", tag="neg_s")
@@ -185,18 +190,22 @@ def tile_attend_gmdn_w_kernel(tc, xT, wl, wm, y, us, tl, tm, wt, offs, out_0, ou
             nc.gpsimd.memset(window[:], 0.0)
             windows.append(window)
 
+        nc.vector.reciprocal(inv_te[:], te[:])
         neg_ms = keep.tile([P, PACK], F32, name="neg_ms")
         tf = keep.tile([P, PACK], F32, name="tf")
         inv_tf = keep.tile([P, PACK], F32, name="inv_tf")
-        f = keep.tile([P, PACK, SLOTS], F32, name="f", tag="a_tl")
+        f = keep.tile([P, PACK, SLOTS], F32, name="f")
         for pair in ((0, 1), (2, 3)):
+            both = slice(pair[0], pair[1] + 1)
+            nc.vector.scalar_tensor_tensor(neg_s[:, both, :], neg_s[:, both, :], 0.5, neg_l[:, both, :], ALU.mult, ALU.add)
+        for t in range(PACK):
+            nc.scalar.activation(e[:, t, :], e[:, t, :], ACT.Copy, scale=inv_te[:, t:t + 1])
+        for pair in ((0, 1), (2, 3)):
+            both = slice(pair[0], pair[1] + 1)
+            nc.vector.tensor_reduce(neg_ms[:, both], neg_s[:, both, :], AXIS.X, ALU.min)
             for t in pair:
-                nc.vector.scalar_tensor_tensor(neg_s[:, t, :], neg_s[:, t, :], 0.5, neg_l[:, t, :], ALU.mult, ALU.add)
-            for t in pair:
-                nc.vector.tensor_reduce(neg_ms[:, t:t + 1], neg_s[:, t, :], AXIS.X, ALU.min)
                 nc.scalar.activation(f[:, t, :], neg_s[:, t, :], ACT.Exp, bias=neg_ms[:, t:t + 1], scale=-1.0,
                                      accum_out=tf[:, t:t + 1])
-                nc.scalar.activation(e[:, t, :], e[:, t, :], ACT.Copy, scale=inv_te[:, t:t + 1])
         for pair in ((0, 1), (2, 3)):
             both = slice(pair[0], pair[1] + 1)
             nc.vector.reciprocal(inv_tf[:, both], tf[:, both])
@@ -234,7 +243,7 @@ def tile_attend_gmdn_w_kernel(tc, xT, wl, wm, y, us, tl, tm, wt, offs, out_0, ou
             for t in range(PACK):
                 nc.tensor.transpose(turned[:, t, :], po_q[:, t, k * P:(k + 1) * P], ident[:])
             nc.scalar.activation(gm_t[:, k, :, :, :], turned[:].rearrange("n (u h) s -> n u s h", h=2), ACT.Copy,
-                                 scale=cols["tm"][:, k:k + 1])
+                                 scale=tm_col[:, k:k + 1])
         for j in range(2, PACK):
             gradient_tile(j, glq, bank_a("d1_%d" % j), j, out_0)
         gm_words = gm_t[:].rearrange("n k u s h -> n (k u s h)").bitcast(F32)

@@ -67,6 +67,11 @@ def tile_attend_gmdn_w_kernel(tc, xT, wl, wm, y, us, tl, tm, wt, offs, out_0, ou
         tm_win = keep.tile([P, COLS], F32, name="tm_win")
         nc.vector.memset(tl_win[:], 0.0)
         nc.vector.memset(tm_win[:], 0.0)
+        windows = []
+        for w in range(WINDOWS):
+            window = keep.tile([P, COLS], F32, name="window%d" % w)
+            nc.vector.memset(window[:], 0.0)
+            windows.append(window)
         x_raw = keep.tile([P, PACK, R], F32, name="x_raw")
 
         nc.scalar.dma_start(out=tl_win[0:1, :], in_=tl[0:1, :])
@@ -148,27 +153,40 @@ def tile_attend_gmdn_w_kernel(tc, xT, wl, wm, y, us, tl, tm, wt, offs, out_0, ou
         wm_pair = keep.tile([P, 2, SLOTS], F32, name="wm_pair", tag="wl_i", align_bytes=64)
         wm_i = keep.tile([P, SLOTS, PACK], BF16, name="wm_i", tag="wm_i", align_bytes=64)
         te = keep.tile([P, PACK], F32, name="te")
-        e = keep.tile([P, PACK, SLOTS], F32, name="e")
-
-        def log_weights(t, neg_l):
-            acc = bank_a("a%d" % t)
-            product(acc, xq_d, E4M3, t, wlq, E4M3)
-            nc.vector.scalar_tensor_tensor(neg_l[:, t, :], flat(acc), neg_us[:, t:t + 1], tl_row[:],
-                                           ALU.mult, ALU.mult)
+        e = keep.tile([P, PACK, SLOTS], F32, name="e", tag="wl_plane2", align_bytes=64)
 
         def weights(t, neg_l, neg_m):
-            nc.vector.tensor_reduce(neg_m[:, t:t + 1], neg_l[:, t, :], AXIS.X, ALU.min)
             nc.scalar.activation(e[:, t, :], neg_l[:, t, :], ACT.Exp, bias=neg_m[:, t:t + 1], scale=-1.0,
                                  accum_out=te[:, t:t + 1])
 
         gather(wm_pair[:, 0, :], "wm", 0)
         neg_l = keep.tile([P, PACK, SLOTS], F32, name="neg_l", tag="wm_plane0", align_bytes=64)
-        for t in range(PACK):
-            log_weights(t, neg_l)
+        for t in range(2):
+            acc = bank_a("a%d" % t)
+            product(acc, xq_d, E4M3, t, wlq, E4M3)
+            nc.vector.scalar_tensor_tensor(neg_l[:, t, :], flat(acc), neg_us[:, t:t + 1], tl_row[:],
+                                           ALU.mult, ALU.mult)
+        a_tl = keep.tile([P, PACK, 2 * P], F32, name="a_tl")
+        for k in range(PACK):
+            acc = bank_b("a_turned%d" % k)
+            cols = slice(k * P, (k + 1) * P)
+            nc.tensor.matmul_mx(
+                out=flat(acc)[:, 0:2 * P], lhsT=wlq[0][:, cols].bitcast(E4M3), lhsT_scale=wlq[1][:, cols],
+                rhs=xq_d[0][:, 2 * P:].bitcast(E4M3), rhs_scale=xq_d[1][:, 2 * P:], start=True, stop=True)
+            nc.scalar.activation(a_tl[:, k, :], flat(acc)[:, 0:2 * P], ACT.Copy, scale=tl_col[:, k:k + 1])
+        backs = [bank_a("l_back%d" % h) for h in range(2)]
+        for k in range(PACK):
+            for h in range(2):
+                nc.tensor.transpose(backs[h][:, k, :], a_tl[:, k, h * P:(h + 1) * P], ident[:])
         gather(wm_pair[:, 1, :], "wm", 1)
         nc.scalar.copy(wm_i[:, :, 0:2], wm_pair[:].rearrange("p j i -> p i j"))
         neg_m = keep.tile([P, PACK], F32, name="neg_m", tag="wm_plane1", align_bytes=64)
-        for t in range(PACK):
+        for t in range(2):
+            nc.vector.tensor_reduce(neg_m[:, t:t + 1], neg_l[:, t, :], AXIS.X, ALU.min)
+            weights(t, neg_l, neg_m)
+        for t in range(2, PACK):
+            nc.vector.tensor_scalar(neg_l[:, t, :], flat(backs[t - 2]), neg_us[:, t:t + 1], None, ALU.mult, ALU.min,
+                                    accum_out=neg_m[:, t:t + 1])
             weights(t, neg_l, neg_m)
         gather(wm_i[:, :, 2], "wm", 2)
         gather(wm_i[:, :, 3], "wm", 3)
@@ -176,7 +194,7 @@ def tile_attend_gmdn_w_kernel(tc, xT, wl, wm, y, us, tl, tm, wt, offs, out_0, ou
         xq_r = quantise("x_r", x_r[:].rearrange("s j p t -> s (j p t)"), E4M3, tag="wm_i")
         inv_te = keep.tile([P, PACK], F32, name="inv_te")
 
-        mean = keep.tile([P, PACK, SLOTS], F32, name="mean")
+        mean = keep.tile([P, PACK, SLOTS], F32, name="mean", tag="wl_plane0", align_bytes=64)
         neg_s = keep.tile([P, PACK, SLOTS], F32, name="neg_s", tag="neg_s")
         for t in range(PACK):
             acc = bank_a("b%d" % t)
@@ -184,17 +202,11 @@ def tile_attend_gmdn_w_kernel(tc, xT, wl, wm, y, us, tl, tm, wt, offs, out_0, ou
             nc.vector.scalar_tensor_tensor(mean[:, t, :], flat(acc), us_sb[:, t:t + 1], tm_row[:], ALU.mult, ALU.mult)
             nc.scalar.activation(neg_s[:, t, :], mean[:, t, :], ACT.Square, bias=neg_y[:, t:t + 1])
 
-        windows = []
-        for tag in ("x_d_scales", "wm_codes", "wm_scales"):
-            window = keep.tile([P, COLS], F32, name="window_" + tag, tag=tag, align_bytes=64)
-            nc.gpsimd.memset(window[:], 0.0)
-            windows.append(window)
-
         nc.vector.reciprocal(inv_te[:], te[:])
         neg_ms = keep.tile([P, PACK], F32, name="neg_ms")
         tf = keep.tile([P, PACK], F32, name="tf")
         inv_tf = keep.tile([P, PACK], F32, name="inv_tf")
-        f = keep.tile([P, PACK, SLOTS], F32, name="f")
+        f = keep.tile([P, PACK, SLOTS], F32, name="f", tag="wl_plane1", align_bytes=64)
         for pair in ((0, 1), (2, 3)):
             both = slice(pair[0], pair[1] + 1)
             nc.vector.scalar_tensor_tensor(neg_s[:, both, :], neg_s[:, both, :], 0.5, neg_l[:, both, :], ALU.mult, ALU.add)

@@ -63,15 +63,10 @@ def tile_attend_gmdn_w_kernel(tc, xT, wl, wm, y, us, tl, tm, wt, offs, out_0, ou
             nc.scalar.dma_start(out=dst[:], in_=src.rearrange("(s t) o -> s (t o)", t=PACK))
 
 
-        tl_win = keep.tile([P, COLS], F32, name="tl_win", tag="tl_win", align_bytes=64)
-        tm_win = keep.tile([P, COLS], F32, name="tm_win")
+        tl_win = keep.tile([P, COLS], F32, name="tl_win", tag="slot_a", align_bytes=64)
+        tm_win = keep.tile([P, COLS], F32, name="tm_win", tag="slot_b", align_bytes=64)
         nc.vector.memset(tl_win[:], 0.0)
         nc.vector.memset(tm_win[:], 0.0)
-        windows = []
-        for w in range(WINDOWS):
-            window = keep.tile([P, COLS], F32, name="window%d" % w)
-            nc.vector.memset(window[:], 0.0)
-            windows.append(window)
         x_raw = keep.tile([P, PACK, R], F32, name="x_raw")
 
         nc.scalar.dma_start(out=tl_win[0:1, :], in_=tl[0:1, :])
@@ -79,13 +74,14 @@ def tile_attend_gmdn_w_kernel(tc, xT, wl, wm, y, us, tl, tm, wt, offs, out_0, ou
         nc.sync.dma_start(out=x_raw[:], in_=xT.rearrange("(p j) r -> p j r", j=PACK))
 
         planes = {}
-        for name, table in (("wl", wl), ("wm", wm)):
-            rows = table.rearrange("(p j) c -> j p c", j=PACK)
-            for j in range(PACK):
-                plane = keep.tile([P, COLS], F32, name="%s_plane%d" % (name, j), tag="%s_plane%d" % (name, j),
-                                  align_bytes=64)
-                nc.sync.dma_start(out=plane[:], in_=rows[j])
-                planes[name, j] = plane
+
+        def load_plane(name, table, j, tag):
+            plane = keep.tile([P, COLS], F32, name="%s_plane%d" % (name, j), tag=tag, align_bytes=64)
+            nc.sync.dma_start(out=plane[:], in_=table.rearrange("(p j) c -> j p c", j=PACK)[j])
+            planes[name, j] = plane
+
+        for j, tag in enumerate(("slot_c", "slot_d", "slot_e", "slot_f")):
+            load_plane("wl", wl, j, tag)
 
         ident = keep.tile([P, P], F32, name="ident")
         make_identity(nc, ident[:])
@@ -115,8 +111,8 @@ def tile_attend_gmdn_w_kernel(tc, xT, wl, wm, y, us, tl, tm, wt, offs, out_0, ou
                 nc.tensor.transpose(turned[:, t, :], x_raw[:, j, t::PACK], ident[:])
             nc.scalar.copy(x_r[:, j, :, :], turned[:].rearrange("s t p -> s p t"))
 
-        def slot_scales(name, win, tag):
-            picked = keep.tile([P, SLOTS], F32, name=name + "_picked", tag=tag, align_bytes=64)
+        def slot_scales(name, win):
+            picked = keep.tile([P, SLOTS], F32, name=name + "_picked")
             nc.vector.tensor_copy(picked[:], win[:].indirect(offsets[:]))
             turned = bank_b(name + "_turned")
             for k in range(PACK):
@@ -134,10 +130,14 @@ def tile_attend_gmdn_w_kernel(tc, xT, wl, wm, y, us, tl, tm, wt, offs, out_0, ou
         wl_i = keep.tile([P, SLOTS, PACK], BF16, name="wl_i", tag="wl_i", align_bytes=64)
         for j in range(PACK):
             turn_x(j)
-        tl_col, tl_spread = slot_scales("tl", tl_win, "tl_picked")
-        tm_col, tm_spread = slot_scales("tm", tm_win, "tl_win")
+        tl_col, tl_spread = slot_scales("tl", tl_win)
+        load_plane("wm", wm, 0, "slot_a")
+        tm_col, tm_spread = slot_scales("tm", tm_win)
+        load_plane("wm", wm, 1, "slot_b")
         gather(wl_i[:, :, 0], "wl", 0)
+        load_plane("wm", wm, 2, "slot_c")
         gather(wl_i[:, :, 1], "wl", 1)
+        load_plane("wm", wm, 3, "slot_d")
         tl_row = keep.tile([P, SLOTS], F32, name="tl_row")
         nc.scalar.copy(tl_row[:], flat(tl_spread))
         tm_row = keep.tile([P, SLOTS], F32, name="tm_row")
@@ -153,14 +153,14 @@ def tile_attend_gmdn_w_kernel(tc, xT, wl, wm, y, us, tl, tm, wt, offs, out_0, ou
         wm_pair = keep.tile([P, 2, SLOTS], F32, name="wm_pair", tag="wl_i", align_bytes=64)
         wm_i = keep.tile([P, SLOTS, PACK], BF16, name="wm_i", tag="wm_i", align_bytes=64)
         te = keep.tile([P, PACK], F32, name="te")
-        e = keep.tile([P, PACK, SLOTS], F32, name="e", tag="wl_plane2", align_bytes=64)
+        e = keep.tile([P, PACK, SLOTS], F32, name="e", tag="slot_e", align_bytes=64)
 
         def weights(t, neg_l, neg_m):
             nc.scalar.activation(e[:, t, :], neg_l[:, t, :], ACT.Exp, bias=neg_m[:, t:t + 1], scale=-1.0,
                                  accum_out=te[:, t:t + 1])
 
         gather(wm_pair[:, 0, :], "wm", 0)
-        neg_l = keep.tile([P, PACK, SLOTS], F32, name="neg_l", tag="wm_plane0", align_bytes=64)
+        neg_l = keep.tile([P, PACK, SLOTS], F32, name="neg_l", tag="slot_a", align_bytes=64)
         for t in range(2):
             acc = bank_a("a%d" % t)
             product(acc, xq_d, E4M3, t, wlq, E4M3)
@@ -180,7 +180,7 @@ def tile_attend_gmdn_w_kernel(tc, xT, wl, wm, y, us, tl, tm, wt, offs, out_0, ou
                 nc.tensor.transpose(backs[h][:, k, :], a_tl[:, k, h * P:(h + 1) * P], ident[:])
         gather(wm_pair[:, 1, :], "wm", 1)
         nc.scalar.copy(wm_i[:, :, 0:2], wm_pair[:].rearrange("p j i -> p i j"))
-        neg_m = keep.tile([P, PACK], F32, name="neg_m", tag="wm_plane1", align_bytes=64)
+        neg_m = keep.tile([P, PACK], F32, name="neg_m", tag="slot_b", align_bytes=64)
         for t in range(2):
             nc.vector.tensor_reduce(neg_m[:, t:t + 1], neg_l[:, t, :], AXIS.X, ALU.min)
             weights(t, neg_l, neg_m)
@@ -190,11 +190,14 @@ def tile_attend_gmdn_w_kernel(tc, xT, wl, wm, y, us, tl, tm, wt, offs, out_0, ou
             weights(t, neg_l, neg_m)
         gather(wm_i[:, :, 2], "wm", 2)
         gather(wm_i[:, :, 3], "wm", 3)
+        inv_te = keep.tile([P, PACK], F32, name="inv_te", tag="slot_d", align_bytes=64)
+        nc.vector.reciprocal(inv_te[:], te[:])
+        for t in range(PACK):
+            nc.scalar.activation(e[:, t, :], e[:, t, :], ACT.Copy, scale=inv_te[:, t:t + 1])
         wmq = quantise("wm", flat(wm_i), E4M3)
         xq_r = quantise("x_r", x_r[:].rearrange("s j p t -> s (j p t)"), E4M3, tag="wm_i")
-        inv_te = keep.tile([P, PACK], F32, name="inv_te")
 
-        mean = keep.tile([P, PACK, SLOTS], F32, name="mean", tag="wl_plane0", align_bytes=64)
+        mean = keep.tile([P, PACK, SLOTS], F32, name="mean", tag="slot_c", align_bytes=64)
         neg_s = keep.tile([P, PACK, SLOTS], F32, name="neg_s", tag="neg_s")
         for t in range(PACK):
             acc = bank_a("b%d" % t)
@@ -202,16 +205,19 @@ def tile_attend_gmdn_w_kernel(tc, xT, wl, wm, y, us, tl, tm, wt, offs, out_0, ou
             nc.vector.scalar_tensor_tensor(mean[:, t, :], flat(acc), us_sb[:, t:t + 1], tm_row[:], ALU.mult, ALU.mult)
             nc.scalar.activation(neg_s[:, t, :], mean[:, t, :], ACT.Square, bias=neg_y[:, t:t + 1])
 
-        nc.vector.reciprocal(inv_te[:], te[:])
+        windows = []
+        for tag in ("x_d_scales", "wm_codes", "wm_scales"):
+            window = keep.tile([P, COLS], F32, name="window_" + tag, tag=tag, align_bytes=64)
+            nc.gpsimd.memset(window[:], 0.0)
+            windows.append(window)
+
         neg_ms = keep.tile([P, PACK], F32, name="neg_ms")
         tf = keep.tile([P, PACK], F32, name="tf")
         inv_tf = keep.tile([P, PACK], F32, name="inv_tf")
-        f = keep.tile([P, PACK, SLOTS], F32, name="f", tag="wl_plane1", align_bytes=64)
+        f = keep.tile([P, PACK, SLOTS], F32, name="f", tag="slot_f", align_bytes=64)
         for pair in ((0, 1), (2, 3)):
             both = slice(pair[0], pair[1] + 1)
             nc.vector.scalar_tensor_tensor(neg_s[:, both, :], neg_s[:, both, :], 0.5, neg_l[:, both, :], ALU.mult, ALU.add)
-        for t in range(PACK):
-            nc.scalar.activation(e[:, t, :], e[:, t, :], ACT.Copy, scale=inv_te[:, t:t + 1])
         for pair in ((0, 1), (2, 3)):
             both = slice(pair[0], pair[1] + 1)
             nc.vector.tensor_reduce(neg_ms[:, both], neg_s[:, both, :], AXIS.X, ALU.min)
@@ -219,24 +225,36 @@ def tile_attend_gmdn_w_kernel(tc, xT, wl, wm, y, us, tl, tm, wt, offs, out_0, ou
                 nc.scalar.activation(f[:, t, :], neg_s[:, t, :], ACT.Exp, bias=neg_ms[:, t:t + 1], scale=-1.0,
                                      accum_out=tf[:, t:t + 1])
         for pair in ((0, 1), (2, 3)):
-            both = slice(pair[0], pair[1] + 1)
-            nc.vector.reciprocal(inv_tf[:, both], tf[:, both])
+            for t in pair:
+                nc.vector.reciprocal(inv_tf[:, t:t + 1], tf[:, t:t + 1])
             for t in pair:
                 nc.vector.scalar_tensor_tensor(e[:, t, :], f[:, t, :], inv_tf[:, t:t + 1], e[:, t, :],
                                                ALU.mult, ALU.subtract)
-        gl = keep.tile([P, SLOTS, PACK], BF16, name="gl", tag="gl", align_bytes=64)
-        nc.vector.tensor_tensor(gl[:].rearrange("p (c i) t -> p c t i", i=2),
-                                e[:].rearrange("p t (c i) -> p c t i", i=2),
-                                tl_wu[:].rearrange("p t (c i) -> p c t i", i=2), ALU.mult)
-        glq = quantise("gl", flat(gl), E5M2)
         q_wu = keep.tile([P, PACK, SLOTS], F32, name="q_wu", tag="neg_s")
-        po_q = keep.tile([P, PACK, SLOTS], F32, name="po_q", tag="gl", align_bytes=64)
         for t in range(PACK):
             nc.scalar.activation(q_wu[:, t, :], mean[:, t, :], ACT.Identity, bias=neg_wuy[:, t:t + 1],
                                  scale=wu[:, t:t + 1])
-        for t in range(PACK):
-            nc.vector.scalar_tensor_tensor(po_q[:, t, :], f[:, t, :], inv_tf[:, t:t + 1], q_wu[:, t, :],
-                                           ALU.mult, ALU.mult)
+
+        def po_times_q(dst, t):
+            nc.vector.scalar_tensor_tensor(dst, f[:, t, :], inv_tf[:, t:t + 1], q_wu[:, t, :], ALU.mult, ALU.mult)
+
+        po_q_first = keep.tile([P, SLOTS], F32, name="po_q_first")
+        po_times_q(po_q_first[:], 0)
+        gl = keep.tile([P, SLOTS, PACK], BF16, name="gl", tag="gl", align_bytes=64)
+        halves = (slice(0, SLOTS // 2), slice(SLOTS // 2, SLOTS))
+        for half in halves:
+            nc.vector.tensor_tensor(gl[:, half, :].rearrange("p (c i) t -> p c t i", i=2),
+                                    e[:, :, half].rearrange("p t (c i) -> p c t i", i=2),
+                                    tl_wu[:, :, half].rearrange("p t (c i) -> p c t i", i=2), ALU.mult)
+        glq = (keep.tile([P, SLOTS], U32, name="gl_codes", align_bytes=64),
+               keep.tile([P, SLOTS], U8, name="gl_scales", align_bytes=64))
+        for half in halves:
+            nc.vector.quantize_mx(out=glq[0][:, half].bitcast(E5M2), scales=glq[1][:, half],
+                                  in_=gl[:, half, :].rearrange("p i t -> p (i t)"))
+        po_q_rest = keep.tile([P, PACK - 1, SLOTS], F32, name="po_q_rest", tag="gl", align_bytes=64)
+        for t in range(1, PACK):
+            po_times_q(po_q_rest[:, t - 1, :], t)
+        po_q = [po_q_first[:]] + [po_q_rest[:, t, :] for t in range(PACK - 1)]
 
         def gradient_tile(n, grad, acc, j, out):
             product(acc, xq_r, E4M3, j, grad, E5M2)
@@ -253,7 +271,7 @@ def tile_attend_gmdn_w_kernel(tc, xT, wl, wm, y, us, tl, tm, wt, offs, out_0, ou
         for k in range(PACK):
             turned = bank_b("gm_turned%d" % k)
             for t in range(PACK):
-                nc.tensor.transpose(turned[:, t, :], po_q[:, t, k * P:(k + 1) * P], ident[:])
+                nc.tensor.transpose(turned[:, t, :], po_q[t][:, k * P:(k + 1) * P], ident[:])
             nc.scalar.activation(gm_t[:, k, :, :, :], turned[:].rearrange("n (u h) s -> n u s h", h=2), ACT.Copy,
                                  scale=tm_col[:, k:k + 1])
         for j in range(2, PACK):

@@ -20,7 +20,9 @@ D = 512
 R = 512
 SLOTS = 512
 COLS = 2048
-WINDOWS = 3
+DIRECT = 2
+TURNED = PACK - DIRECT
+PAIRS = ((0, 1), (2, 3))
 
 FLOPS = 4 * 2 * D * R * SLOTS
 
@@ -29,9 +31,9 @@ def tile_attend_gmdn_w_kernel(tc, xT, wl, wm, y, us, tl, tm, wt, offs, out_0, ou
     nc = tc.nc
     with ExitStack() as ctx:
         keep = ctx.enter_context(tc.tile_pool(name="keep", bufs=1))
-        stage = ctx.enter_context(tc.tile_pool(name="stage", bufs=4))
-        psum_a = ctx.enter_context(tc.psum_pool(name="psum_a", bufs=4))
-        psum_b = ctx.enter_context(tc.psum_pool(name="psum_b", bufs=4))
+        stage = ctx.enter_context(tc.tile_pool(name="stage", bufs=PACK))
+        psum_a = ctx.enter_context(tc.psum_pool(name="psum_a", bufs=PACK))
+        psum_b = ctx.enter_context(tc.psum_pool(name="psum_b", bufs=PACK))
 
         def bank_a(name):
             return psum_a.tile([P, PACK, P], F32, name=name, tag="a")
@@ -39,8 +41,8 @@ def tile_attend_gmdn_w_kernel(tc, xT, wl, wm, y, us, tl, tm, wt, offs, out_0, ou
         def bank_b(name):
             return psum_b.tile([P, PACK, P], F32, name=name, tag="b")
 
-        def flat(t):
-            return t[:].rearrange("p a b -> p (a b)")
+        def flat(tile):
+            return tile[:].rearrange("p a b -> p (a b)")
 
         def quantise(name, src, fmt, tag=None):
             codes = keep.tile([P, SLOTS], U32, name=name + "_codes", tag=tag or name + "_codes", align_bytes=64)
@@ -48,11 +50,11 @@ def tile_attend_gmdn_w_kernel(tc, xT, wl, wm, y, us, tl, tm, wt, offs, out_0, ou
             nc.vector.quantize_mx(out=codes[:].bitcast(fmt), scales=scales[:], in_=src)
             return codes, scales
 
-        def product(acc, stat, stat_fmt, j, mov, mov_fmt):
-            cols = slice(j * P, (j + 1) * P)
+        def product(acc, x_quantised, block, moving, moving_fmt):
+            cols = slice(block * P, (block + 1) * P)
             nc.tensor.matmul_mx(
-                out=flat(acc), lhsT=stat[0][:, cols].bitcast(stat_fmt), lhsT_scale=stat[1][:, cols],
-                rhs=mov[0][:].bitcast(mov_fmt), rhs_scale=mov[1][:], start=True, stop=True)
+                out=flat(acc), lhsT=x_quantised[0][:, cols].bitcast(E4M3), lhsT_scale=x_quantised[1][:, cols],
+                rhs=moving[0][:].bitcast(moving_fmt), rhs_scale=moving[1][:], start=True, stop=True)
 
         offsets = keep.tile([P, SLOTS // 16], U16, name="offsets")
         nc.sync.dma_start(offsets[:], offs)
@@ -62,13 +64,11 @@ def tile_attend_gmdn_w_kernel(tc, xT, wl, wm, y, us, tl, tm, wt, offs, out_0, ou
         for dst, src in ((us_sb, us), (wt_sb, wt), (y_sb, y)):
             nc.scalar.dma_start(out=dst[:], in_=src.rearrange("(s t) o -> s (t o)", t=PACK))
 
-
         tl_win = keep.tile([P, COLS], F32, name="tl_win", tag="slot_a", align_bytes=64)
         tm_win = keep.tile([P, COLS], F32, name="tm_win", tag="slot_b", align_bytes=64)
         nc.vector.memset(tl_win[:], 0.0)
         nc.vector.memset(tm_win[:], 0.0)
         x_raw = keep.tile([P, PACK, R], F32, name="x_raw")
-
         nc.scalar.dma_start(out=tl_win[0:1, :], in_=tl[0:1, :])
         nc.scalar.dma_start(out=tm_win[0:1, :], in_=tm[0:1, :])
         nc.sync.dma_start(out=x_raw[:], in_=xT.rearrange("(p j) r -> p j r", j=PACK))
@@ -85,9 +85,6 @@ def tile_attend_gmdn_w_kernel(tc, xT, wl, wm, y, us, tl, tm, wt, offs, out_0, ou
 
         ident = keep.tile([P, P], F32, name="ident")
         make_identity(nc, ident[:])
-
-        warm = keep.tile([P, 2], F32, name="warm")
-        nc.scalar.activation(warm[:], ident[:, 0:2], ACT.Exp)
 
         neg_us = keep.tile([P, PACK], F32, name="neg_us")
         neg_y = keep.tile([P, PACK], F32, name="neg_y")
@@ -119,10 +116,10 @@ def tile_attend_gmdn_w_kernel(tc, xT, wl, wm, y, us, tl, tm, wt, offs, out_0, ou
                 nc.tensor.transpose(turned[:, k, :], picked[:, k * P:(k + 1) * P], ident[:])
             col = keep.tile([P, PACK], F32, name=name + "_col")
             nc.scalar.copy(col[:], turned[:, :, 0])
-            row = bank_b(name + "_row")
+            spread = bank_b(name + "_row")
             for k in range(PACK):
-                nc.tensor.transpose(row[:, k, :], col[:, k:k + 1].to_broadcast([P, P]), ident[:])
-            return col, row
+                nc.tensor.transpose(spread[:, k, :], col[:, k:k + 1].to_broadcast([P, P]), ident[:])
+            return col, spread
 
         def gather(dst, name, j):
             nc.vector.tensor_copy(dst, planes[name, j][:].indirect(offsets[:]))
@@ -142,9 +139,9 @@ def tile_attend_gmdn_w_kernel(tc, xT, wl, wm, y, us, tl, tm, wt, offs, out_0, ou
         nc.scalar.copy(tl_row[:], flat(tl_spread))
         tm_row = keep.tile([P, SLOTS], F32, name="tm_row")
         nc.scalar.copy(tm_row[:], flat(tm_spread))
-        tl_wu = keep.tile([P, PACK, SLOTS], F32, name="tl_wu")
+        neg_tl_wu = keep.tile([P, PACK, SLOTS], F32, name="tl_wu")
         for t in range(PACK):
-            nc.scalar.activation(tl_wu[:, t, :], flat(tl_spread), ACT.Copy, scale=neg_wu[:, t:t + 1])
+            nc.scalar.activation(neg_tl_wu[:, t, :], flat(tl_spread), ACT.Copy, scale=neg_wu[:, t:t + 1])
         xq_d = quantise("x_d", x_d[:].rearrange("p t s j -> p (t s j)"), E4M3)
         gather(wl_i[:, :, 2], "wl", 2)
         gather(wl_i[:, :, 3], "wl", 3)
@@ -155,55 +152,53 @@ def tile_attend_gmdn_w_kernel(tc, xT, wl, wm, y, us, tl, tm, wt, offs, out_0, ou
         te = keep.tile([P, PACK], F32, name="te")
         e = keep.tile([P, PACK, SLOTS], F32, name="e", tag="slot_e", align_bytes=64)
 
-        def weights(t, neg_l, neg_m):
-            nc.scalar.activation(e[:, t, :], neg_l[:, t, :], ACT.Exp, bias=neg_m[:, t:t + 1], scale=-1.0,
-                                 accum_out=te[:, t:t + 1])
-
         gather(wm_pair[:, 0, :], "wm", 0)
         neg_l = keep.tile([P, PACK, SLOTS], F32, name="neg_l", tag="slot_a", align_bytes=64)
-        for t in range(2):
+        for t in range(DIRECT):
             acc = bank_a("a%d" % t)
-            product(acc, xq_d, E4M3, t, wlq, E4M3)
+            product(acc, xq_d, t, wlq, E4M3)
             nc.vector.scalar_tensor_tensor(neg_l[:, t, :], flat(acc), neg_us[:, t:t + 1], tl_row[:],
                                            ALU.mult, ALU.mult)
-        a_tl = keep.tile([P, PACK, 2 * P], F32, name="a_tl")
+        a_tl = keep.tile([P, PACK, TURNED * P], F32, name="a_tl")
         for k in range(PACK):
-            acc = bank_b("a_turned%d" % k)
-            cols = slice(k * P, (k + 1) * P)
+            acc = flat(bank_b("a_turned%d" % k))[:, 0:TURNED * P]
+            quarter = slice(k * P, (k + 1) * P)
             nc.tensor.matmul_mx(
-                out=flat(acc)[:, 0:2 * P], lhsT=wlq[0][:, cols].bitcast(E4M3), lhsT_scale=wlq[1][:, cols],
-                rhs=xq_d[0][:, 2 * P:].bitcast(E4M3), rhs_scale=xq_d[1][:, 2 * P:], start=True, stop=True)
-            nc.scalar.activation(a_tl[:, k, :], flat(acc)[:, 0:2 * P], ACT.Copy, scale=tl_col[:, k:k + 1])
-        backs = [bank_a("l_back%d" % h) for h in range(2)]
+                out=acc, lhsT=wlq[0][:, quarter].bitcast(E4M3), lhsT_scale=wlq[1][:, quarter],
+                rhs=xq_d[0][:, DIRECT * P:].bitcast(E4M3), rhs_scale=xq_d[1][:, DIRECT * P:], start=True, stop=True)
+            nc.scalar.activation(a_tl[:, k, :], acc, ACT.Copy, scale=tl_col[:, k:k + 1])
+        a_tl_back = [bank_a("l_back%d" % n) for n in range(TURNED)]
         for k in range(PACK):
-            for h in range(2):
-                nc.tensor.transpose(backs[h][:, k, :], a_tl[:, k, h * P:(h + 1) * P], ident[:])
+            for n in range(TURNED):
+                nc.tensor.transpose(a_tl_back[n][:, k, :], a_tl[:, k, n * P:(n + 1) * P], ident[:])
         gather(wm_pair[:, 1, :], "wm", 1)
         nc.scalar.copy(wm_i[:, :, 0:2], wm_pair[:].rearrange("p j i -> p i j"))
         neg_m = keep.tile([P, PACK], F32, name="neg_m", tag="slot_b", align_bytes=64)
-        for t in range(2):
-            nc.vector.tensor_reduce(neg_m[:, t:t + 1], neg_l[:, t, :], AXIS.X, ALU.min)
-            weights(t, neg_l, neg_m)
-        for t in range(2, PACK):
-            nc.vector.tensor_scalar(neg_l[:, t, :], flat(backs[t - 2]), neg_us[:, t:t + 1], None, ALU.mult, ALU.min,
-                                    accum_out=neg_m[:, t:t + 1])
-            weights(t, neg_l, neg_m)
+        for t in range(PACK):
+            if t < DIRECT:
+                nc.vector.tensor_reduce(neg_m[:, t:t + 1], neg_l[:, t, :], AXIS.X, ALU.min)
+            else:
+                nc.vector.tensor_scalar(neg_l[:, t, :], flat(a_tl_back[t - DIRECT]), neg_us[:, t:t + 1], None,
+                                        ALU.mult, ALU.min, accum_out=neg_m[:, t:t + 1])
+            nc.scalar.activation(e[:, t, :], neg_l[:, t, :], ACT.Exp, bias=neg_m[:, t:t + 1], scale=-1.0,
+                                 accum_out=te[:, t:t + 1])
         gather(wm_i[:, :, 2], "wm", 2)
         gather(wm_i[:, :, 3], "wm", 3)
         inv_te = keep.tile([P, PACK], F32, name="inv_te", tag="slot_d", align_bytes=64)
         nc.vector.reciprocal(inv_te[:], te[:])
+        prior = e
         for t in range(PACK):
-            nc.scalar.activation(e[:, t, :], e[:, t, :], ACT.Copy, scale=inv_te[:, t:t + 1])
+            nc.scalar.activation(prior[:, t, :], e[:, t, :], ACT.Copy, scale=inv_te[:, t:t + 1])
         wmq = quantise("wm", flat(wm_i), E4M3)
         xq_r = quantise("x_r", x_r[:].rearrange("s j p t -> s (j p t)"), E4M3, tag="wm_i")
 
         mean = keep.tile([P, PACK, SLOTS], F32, name="mean", tag="slot_c", align_bytes=64)
-        neg_s = keep.tile([P, PACK, SLOTS], F32, name="neg_s", tag="neg_s")
+        q_squared = keep.tile([P, PACK, SLOTS], F32, name="neg_s", tag="neg_s")
         for t in range(PACK):
             acc = bank_a("b%d" % t)
-            product(acc, xq_d, E4M3, t, wmq, E4M3)
+            product(acc, xq_d, t, wmq, E4M3)
             nc.vector.scalar_tensor_tensor(mean[:, t, :], flat(acc), us_sb[:, t:t + 1], tm_row[:], ALU.mult, ALU.mult)
-            nc.scalar.activation(neg_s[:, t, :], mean[:, t, :], ACT.Square, bias=neg_y[:, t:t + 1])
+            nc.scalar.activation(q_squared[:, t, :], mean[:, t, :], ACT.Square, bias=neg_y[:, t:t + 1])
 
         windows = []
         for tag in ("x_d_scales", "wm_codes", "wm_scales"):
@@ -215,21 +210,24 @@ def tile_attend_gmdn_w_kernel(tc, xT, wl, wm, y, us, tl, tm, wt, offs, out_0, ou
         tf = keep.tile([P, PACK], F32, name="tf")
         inv_tf = keep.tile([P, PACK], F32, name="inv_tf")
         f = keep.tile([P, PACK, SLOTS], F32, name="f", tag="slot_f", align_bytes=64)
-        for pair in ((0, 1), (2, 3)):
+        neg_s = q_squared
+        for pair in PAIRS:
             both = slice(pair[0], pair[1] + 1)
-            nc.vector.scalar_tensor_tensor(neg_s[:, both, :], neg_s[:, both, :], 0.5, neg_l[:, both, :], ALU.mult, ALU.add)
-        for pair in ((0, 1), (2, 3)):
+            nc.vector.scalar_tensor_tensor(neg_s[:, both, :], q_squared[:, both, :], 0.5, neg_l[:, both, :],
+                                           ALU.mult, ALU.add)
+        for pair in PAIRS:
             both = slice(pair[0], pair[1] + 1)
             nc.vector.tensor_reduce(neg_ms[:, both], neg_s[:, both, :], AXIS.X, ALU.min)
             for t in pair:
                 nc.scalar.activation(f[:, t, :], neg_s[:, t, :], ACT.Exp, bias=neg_ms[:, t:t + 1], scale=-1.0,
                                      accum_out=tf[:, t:t + 1])
-        for pair in ((0, 1), (2, 3)):
+        po_less_prior = prior
+        for pair in PAIRS:
             for t in pair:
                 nc.vector.reciprocal(inv_tf[:, t:t + 1], tf[:, t:t + 1])
             for t in pair:
-                nc.vector.scalar_tensor_tensor(e[:, t, :], f[:, t, :], inv_tf[:, t:t + 1], e[:, t, :],
-                                               ALU.mult, ALU.subtract)
+                nc.vector.scalar_tensor_tensor(po_less_prior[:, t, :], f[:, t, :], inv_tf[:, t:t + 1],
+                                               prior[:, t, :], ALU.mult, ALU.subtract)
         q_wu = keep.tile([P, PACK, SLOTS], F32, name="q_wu", tag="neg_s")
         for t in range(PACK):
             nc.scalar.activation(q_wu[:, t, :], mean[:, t, :], ACT.Identity, bias=neg_wuy[:, t:t + 1],
@@ -244,8 +242,8 @@ def tile_attend_gmdn_w_kernel(tc, xT, wl, wm, y, us, tl, tm, wt, offs, out_0, ou
         halves = (slice(0, SLOTS // 2), slice(SLOTS // 2, SLOTS))
         for half in halves:
             nc.vector.tensor_tensor(gl[:, half, :].rearrange("p (c i) t -> p c t i", i=2),
-                                    e[:, :, half].rearrange("p t (c i) -> p c t i", i=2),
-                                    tl_wu[:, :, half].rearrange("p t (c i) -> p c t i", i=2), ALU.mult)
+                                    po_less_prior[:, :, half].rearrange("p t (c i) -> p c t i", i=2),
+                                    neg_tl_wu[:, :, half].rearrange("p t (c i) -> p c t i", i=2), ALU.mult)
         glq = (keep.tile([P, SLOTS], U32, name="gl_codes", align_bytes=64),
                keep.tile([P, SLOTS], U8, name="gl_scales", align_bytes=64))
         for half in halves:
@@ -254,19 +252,20 @@ def tile_attend_gmdn_w_kernel(tc, xT, wl, wm, y, us, tl, tm, wt, offs, out_0, ou
         po_q_rest = keep.tile([P, PACK - 1, SLOTS], F32, name="po_q_rest", tag="gl", align_bytes=64)
         for t in range(1, PACK):
             po_times_q(po_q_rest[:, t - 1, :], t)
-        po_q = [po_q_first[:]] + [po_q_rest[:, t, :] for t in range(PACK - 1)]
+        po_q = [po_q_first[:]] + [po_q_rest[:, n, :] for n in range(PACK - 1)]
 
-        def gradient_tile(n, grad, acc, j, out):
-            product(acc, xq_r, E4M3, j, grad, E5M2)
+        def gradient_tile(window, grad, acc, j, out):
+            product(acc, xq_r, j, grad, E5M2)
             staged = stage.tile([P, SLOTS], F32, name="staged")
             nc.scalar.copy(staged[:], flat(acc))
-            window = windows[n % WINDOWS]
             nc.vector.tensor_copy(window[:].indirect(offsets[:]), staged[:])
             nc.sync.dma_start(out=out.rearrange("(p j) c -> j p c", j=PACK)[j], in_=window[:])
 
-        for j in range(2):
-            gradient_tile(j, glq, bank_a("d1_%d" % j), j, out_0)
+        def window_of(tile_number):
+            return windows[tile_number % len(windows)]
 
+        for j in range(PACK // 2):
+            gradient_tile(window_of(j), glq, bank_a("d1_%d" % j), j, out_0)
         gm_t = keep.tile([P, PACK, 2, P, 2], BF16, name="gm_t")
         for k in range(PACK):
             turned = bank_b("gm_turned%d" % k)
@@ -274,17 +273,18 @@ def tile_attend_gmdn_w_kernel(tc, xT, wl, wm, y, us, tl, tm, wt, offs, out_0, ou
                 nc.tensor.transpose(turned[:, t, :], po_q[t][:, k * P:(k + 1) * P], ident[:])
             nc.scalar.activation(gm_t[:, k, :, :, :], turned[:].rearrange("n (u h) s -> n u s h", h=2), ACT.Copy,
                                  scale=tm_col[:, k:k + 1])
-        for j in range(2, PACK):
-            gradient_tile(j, glq, bank_a("d1_%d" % j), j, out_0)
-        gm_words = gm_t[:].rearrange("n k u s h -> n (k u s h)").bitcast(F32)
+        for j in range(PACK // 2, PACK):
+            gradient_tile(window_of(j), glq, bank_a("d1_%d" % j), j, out_0)
+        gm_t_words = gm_t[:].rearrange("n k u s h -> n (k u s h)").bitcast(F32)
         gm = keep.tile([P, SLOTS, PACK], BF16, name="gm", align_bytes=64)
-        gm_pairs = flat(gm).bitcast(F32).rearrange("s (k n u) -> s k n u", k=PACK, u=2)
-        for half in range(2):
-            back = bank_b("gm_back%d" % half)
-            for c in range(PACK):
-                w0 = (PACK * half + c) * P
-                nc.tensor.transpose(back[:, c, :], gm_words[:, w0:w0 + P], ident[:])
-            nc.scalar.copy(gm_pairs[:, 2 * half:2 * half + 2, :, :], back[:].rearrange("s (k u) n -> s k n u", u=2))
+        gm_words = flat(gm).bitcast(F32).rearrange("s (k n u) -> s k n u", k=PACK, u=2)
+        for k0 in range(0, PACK, 2):
+            back = bank_b("gm_back%d" % (k0 // 2))
+            for block in range(PACK):
+                first = (2 * k0 + block) * P
+                nc.tensor.transpose(back[:, block, :], gm_t_words[:, first:first + P], ident[:])
+            nc.scalar.copy(gm_words[:, k0:k0 + 2, :, :], back[:].rearrange("s (k u) n -> s k n u", u=2))
         gmq = quantise("gm", flat(gm), E5M2)
+
         for j in range(PACK):
-            gradient_tile(PACK + j, gmq, bank_b("d2_%d" % j), j, out_1)
+            gradient_tile(window_of(PACK + j), gmq, bank_b("d2_%d" % j), j, out_1)

from contextlib import ExitStack

import concourse.mybir as mybir
from concourse.masks import make_identity

F32 = mybir.dt.float32
BF16 = mybir.dt.bfloat16
U32 = mybir.dt.uint32
U16 = mybir.dt.uint16
U8 = mybir.dt.uint8
E4M3 = mybir.dt.float8_e4m3fn_x4
E5M2 = mybir.dt.float8_e5m2_x4
ALU = mybir.AluOpType
ACT = mybir.ActivationFunctionType
AXIS = mybir.AxisListType

P = 128
PACK = 4
D = 512
R = 512
SLOTS = 512
COLS = 2048
DIRECT = 2
TURNED = PACK - DIRECT
PAIRS = ((0, 1), (2, 3))

FLOPS = 4 * 2 * D * R * SLOTS


def tile_attend_gmdn_w_kernel(tc, xT, wl, wm, y, us, tl, tm, wt, offs, out_0, out_1):
    nc = tc.nc
    with ExitStack() as ctx:
        keep = ctx.enter_context(tc.tile_pool(name="keep", bufs=1))
        stage = ctx.enter_context(tc.tile_pool(name="stage", bufs=PACK))
        psum_a = ctx.enter_context(tc.psum_pool(name="psum_a", bufs=PACK))
        psum_b = ctx.enter_context(tc.psum_pool(name="psum_b", bufs=PACK))

        def bank_a(name):
            return psum_a.tile([P, PACK, P], F32, name=name, tag="a")

        def bank_b(name):
            return psum_b.tile([P, PACK, P], F32, name=name, tag="b")

        def flat(tile):
            return tile[:].rearrange("p a b -> p (a b)")

        def quantise(name, src, fmt, tag=None):
            codes = keep.tile([P, SLOTS], U32, name=name + "_codes", tag=tag or name + "_codes", align_bytes=64)
            scales = keep.tile([P, SLOTS], U8, name=name + "_scales", tag=name + "_scales", align_bytes=64)
            nc.vector.quantize_mx(out=codes[:].bitcast(fmt), scales=scales[:], in_=src)
            return codes, scales

        def product(acc, x_quantised, block, moving, moving_fmt):
            cols = slice(block * P, (block + 1) * P)
            nc.tensor.matmul_mx(
                out=flat(acc), lhsT=x_quantised[0][:, cols].bitcast(E4M3), lhsT_scale=x_quantised[1][:, cols],
                rhs=moving[0][:].bitcast(moving_fmt), rhs_scale=moving[1][:], start=True, stop=True)

        offsets = keep.tile([P, SLOTS // 16], U16, name="offsets")
        nc.sync.dma_start(offsets[:], offs)
        y_sb = keep.tile([P, PACK], F32, name="y_sb")
        us_sb = keep.tile([P, PACK], F32, name="us_sb")
        wt_sb = keep.tile([P, PACK], F32, name="wt_sb")
        for dst, src in ((us_sb, us), (wt_sb, wt), (y_sb, y)):
            nc.scalar.dma_start(out=dst[:], in_=src.rearrange("(s t) o -> s (t o)", t=PACK))

        tl_win = keep.tile([P, COLS], F32, name="tl_win", tag="slot_a", align_bytes=64)
        tm_win = keep.tile([P, COLS], F32, name="tm_win", tag="slot_b", align_bytes=64)
        nc.vector.memset(tl_win[:], 0.0)
        nc.vector.memset(tm_win[:], 0.0)
        x_raw = keep.tile([P, PACK, R], F32, name="x_raw")
        nc.scalar.dma_start(out=tl_win[0:1, :], in_=tl[0:1, :])
        nc.scalar.dma_start(out=tm_win[0:1, :], in_=tm[0:1, :])
        nc.sync.dma_start(out=x_raw[:], in_=xT.rearrange("(p j) r -> p j r", j=PACK))

        planes = {}

        def load_plane(name, table, j, tag):
            plane = keep.tile([P, COLS], F32, name="%s_plane%d" % (name, j), tag=tag, align_bytes=64)
            nc.sync.dma_start(out=plane[:], in_=table.rearrange("(p j) c -> j p c", j=PACK)[j])
            planes[name, j] = plane

        for j, tag in enumerate(("slot_c", "slot_d", "slot_e", "slot_f")):
            load_plane("wl", wl, j, tag)

        ident = keep.tile([P, P], F32, name="ident")
        make_identity(nc, ident[:])

        neg_us = keep.tile([P, PACK], F32, name="neg_us")
        neg_y = keep.tile([P, PACK], F32, name="neg_y")
        wu = keep.tile([P, PACK], F32, name="wu")
        neg_wu = keep.tile([P, PACK], F32, name="neg_wu")
        neg_wuy = keep.tile([P, PACK], F32, name="neg_wuy")
        nc.gpsimd.tensor_scalar(neg_us[:], us_sb[:], -1.0, 0.0, ALU.mult, ALU.add)
        nc.gpsimd.tensor_scalar(neg_y[:], y_sb[:], -1.0, 0.0, ALU.mult, ALU.add)
        nc.gpsimd.tensor_tensor(wu[:], wt_sb[:], us_sb[:], ALU.mult)
        nc.gpsimd.tensor_tensor(neg_wu[:], wt_sb[:], neg_us[:], ALU.mult)
        nc.gpsimd.tensor_tensor(neg_wuy[:], wu[:], neg_y[:], ALU.mult)

        x_d = keep.tile([P, PACK, P, PACK], BF16, name="x_d", align_bytes=64)
        nc.scalar.copy(x_d[:], x_raw[:].rearrange("p j (s t) -> p t s j", t=PACK))

        x_r = keep.tile([P, PACK, P, PACK], BF16, name="x_r", align_bytes=64)

        def turn_x(j):
            turned = bank_a("x_turned%d" % j)
            for t in range(PACK):
                nc.tensor.transpose(turned[:, t, :], x_raw[:, j, t::PACK], ident[:])
            nc.scalar.copy(x_r[:, j, :, :], turned[:].rearrange("s t p -> s p t"))

        def slot_scales(name, win):
            picked = keep.tile([P, SLOTS], F32, name=name + "_picked")
            nc.vector.tensor_copy(picked[:], win[:].indirect(offsets[:]))
            turned = bank_b(name + "_turned")
            for k in range(PACK):
                nc.tensor.transpose(turned[:, k, :], picked[:, k * P:(k + 1) * P], ident[:])
            col = keep.tile([P, PACK], F32, name=name + "_col")
            nc.scalar.copy(col[:], turned[:, :, 0])
            spread = bank_b(name + "_row")
            for k in range(PACK):
                nc.tensor.transpose(spread[:, k, :], col[:, k:k + 1].to_broadcast([P, P]), ident[:])
            return col, spread

        def gather(dst, name, j):
            nc.vector.tensor_copy(dst, planes[name, j][:].indirect(offsets[:]))

        wl_i = keep.tile([P, SLOTS, PACK], BF16, name="wl_i", tag="wl_i", align_bytes=64)
        for j in range(PACK):
            turn_x(j)
        tl_col, tl_spread = slot_scales("tl", tl_win)
        load_plane("wm", wm, 0, "slot_a")
        tm_col, tm_spread = slot_scales("tm", tm_win)
        load_plane("wm", wm, 1, "slot_b")
        gather(wl_i[:, :, 0], "wl", 0)
        load_plane("wm", wm, 2, "slot_c")
        gather(wl_i[:, :, 1], "wl", 1)
        load_plane("wm", wm, 3, "slot_d")
        tl_row = keep.tile([P, SLOTS], F32, name="tl_row")
        nc.scalar.copy(tl_row[:], flat(tl_spread))
        tm_row = keep.tile([P, SLOTS], F32, name="tm_row")
        nc.scalar.copy(tm_row[:], flat(tm_spread))
        neg_tl_wu = keep.tile([P, PACK, SLOTS], F32, name="tl_wu")
        for t in range(PACK):
            nc.scalar.activation(neg_tl_wu[:, t, :], flat(tl_spread), ACT.Copy, scale=neg_wu[:, t:t + 1])
        xq_d = quantise("x_d", x_d[:].rearrange("p t s j -> p (t s j)"), E4M3)
        gather(wl_i[:, :, 2], "wl", 2)
        gather(wl_i[:, :, 3], "wl", 3)
        wlq = quantise("wl", flat(wl_i), E4M3)

        wm_pair = keep.tile([P, 2, SLOTS], F32, name="wm_pair", tag="wl_i", align_bytes=64)
        wm_i = keep.tile([P, SLOTS, PACK], BF16, name="wm_i", tag="wm_i", align_bytes=64)
        te = keep.tile([P, PACK], F32, name="te")
        e = keep.tile([P, PACK, SLOTS], F32, name="e", tag="slot_e", align_bytes=64)

        gather(wm_pair[:, 0, :], "wm", 0)
        neg_l = keep.tile([P, PACK, SLOTS], F32, name="neg_l", tag="slot_a", align_bytes=64)
        for t in range(DIRECT):
            acc = bank_a("a%d" % t)
            product(acc, xq_d, t, wlq, E4M3)
            nc.vector.scalar_tensor_tensor(neg_l[:, t, :], flat(acc), neg_us[:, t:t + 1], tl_row[:],
                                           ALU.mult, ALU.mult)
        a_tl = keep.tile([P, PACK, TURNED * P], F32, name="a_tl")
        for k in range(PACK):
            acc = flat(bank_b("a_turned%d" % k))[:, 0:TURNED * P]
            quarter = slice(k * P, (k + 1) * P)
            nc.tensor.matmul_mx(
                out=acc, lhsT=wlq[0][:, quarter].bitcast(E4M3), lhsT_scale=wlq[1][:, quarter],
                rhs=xq_d[0][:, DIRECT * P:].bitcast(E4M3), rhs_scale=xq_d[1][:, DIRECT * P:], start=True, stop=True)
            nc.scalar.activation(a_tl[:, k, :], acc, ACT.Copy, scale=tl_col[:, k:k + 1])
        a_tl_back = [bank_a("l_back%d" % n) for n in range(TURNED)]
        for k in range(PACK):
            for n in range(TURNED):
                nc.tensor.transpose(a_tl_back[n][:, k, :], a_tl[:, k, n * P:(n + 1) * P], ident[:])
        gather(wm_pair[:, 1, :], "wm", 1)
        nc.scalar.copy(wm_i[:, :, 0:2], wm_pair[:].rearrange("p j i -> p i j"))
        neg_m = keep.tile([P, PACK], F32, name="neg_m", tag="slot_b", align_bytes=64)
        for t in range(PACK):
            if t < DIRECT:
                nc.vector.tensor_reduce(neg_m[:, t:t + 1], neg_l[:, t, :], AXIS.X, ALU.min)
            else:
                nc.vector.tensor_scalar(neg_l[:, t, :], flat(a_tl_back[t - DIRECT]), neg_us[:, t:t + 1], None,
                                        ALU.mult, ALU.min, accum_out=neg_m[:, t:t + 1])
            nc.scalar.activation(e[:, t, :], neg_l[:, t, :], ACT.Exp, bias=neg_m[:, t:t + 1], scale=-1.0,
                                 accum_out=te[:, t:t + 1])
        gather(wm_i[:, :, 2], "wm", 2)
        gather(wm_i[:, :, 3], "wm", 3)
        inv_te = keep.tile([P, PACK], F32, name="inv_te", tag="slot_d", align_bytes=64)
        nc.vector.reciprocal(inv_te[:], te[:])
        prior = e
        for t in range(PACK):
            nc.scalar.activation(prior[:, t, :], e[:, t, :], ACT.Copy, scale=inv_te[:, t:t + 1])
        wmq = quantise("wm", flat(wm_i), E4M3)
        xq_r = quantise("x_r", x_r[:].rearrange("s j p t -> s (j p t)"), E4M3, tag="wm_i")

        mean = keep.tile([P, PACK, SLOTS], F32, name="mean", tag="slot_c", align_bytes=64)
        q_squared = keep.tile([P, PACK, SLOTS], F32, name="neg_s", tag="neg_s")
        for t in range(PACK):
            acc = bank_a("b%d" % t)
            product(acc, xq_d, t, wmq, E4M3)
            nc.vector.scalar_tensor_tensor(mean[:, t, :], flat(acc), us_sb[:, t:t + 1], tm_row[:], ALU.mult, ALU.mult)
            nc.scalar.activation(q_squared[:, t, :], mean[:, t, :], ACT.Square, bias=neg_y[:, t:t + 1])

        windows = []
        for tag in ("x_d_scales", "wm_codes", "wm_scales"):
            window = keep.tile([P, COLS], F32, name="window_" + tag, tag=tag, align_bytes=64)
            nc.gpsimd.memset(window[:], 0.0)
            windows.append(window)

        neg_ms = keep.tile([P, PACK], F32, name="neg_ms")
        tf = keep.tile([P, PACK], F32, name="tf")
        inv_tf = keep.tile([P, PACK], F32, name="inv_tf")
        f = keep.tile([P, PACK, SLOTS], F32, name="f", tag="slot_f", align_bytes=64)
        neg_s = q_squared
        for pair in PAIRS:
            both = slice(pair[0], pair[1] + 1)
            nc.vector.scalar_tensor_tensor(neg_s[:, both, :], q_squared[:, both, :], 0.5, neg_l[:, both, :],
                                           ALU.mult, ALU.add)
        for pair in PAIRS:
            both = slice(pair[0], pair[1] + 1)
            nc.vector.tensor_reduce(neg_ms[:, both], neg_s[:, both, :], AXIS.X, ALU.min)
            for t in pair:
                nc.scalar.activation(f[:, t, :], neg_s[:, t, :], ACT.Exp, bias=neg_ms[:, t:t + 1], scale=-1.0,
                                     accum_out=tf[:, t:t + 1])
        po_less_prior = prior
        for pair in PAIRS:
            for t in pair:
                nc.vector.reciprocal(inv_tf[:, t:t + 1], tf[:, t:t + 1])
            for t in pair:
                nc.vector.scalar_tensor_tensor(po_less_prior[:, t, :], f[:, t, :], inv_tf[:, t:t + 1],
                                               prior[:, t, :], ALU.mult, ALU.subtract)
        q_wu = keep.tile([P, PACK, SLOTS], F32, name="q_wu", tag="neg_s")
        for t in range(PACK):
            nc.scalar.activation(q_wu[:, t, :], mean[:, t, :], ACT.Identity, bias=neg_wuy[:, t:t + 1],
                                 scale=wu[:, t:t + 1])

        def po_times_q(dst, t):
            nc.vector.scalar_tensor_tensor(dst, f[:, t, :], inv_tf[:, t:t + 1], q_wu[:, t, :], ALU.mult, ALU.mult)

        po_q_first = keep.tile([P, SLOTS], F32, name="po_q_first")
        po_times_q(po_q_first[:], 0)
        gl = keep.tile([P, SLOTS, PACK], BF16, name="gl", tag="gl", align_bytes=64)
        halves = (slice(0, SLOTS // 2), slice(SLOTS // 2, SLOTS))
        for half in halves:
            nc.vector.tensor_tensor(gl[:, half, :].rearrange("p (c i) t -> p c t i", i=2),
                                    po_less_prior[:, :, half].rearrange("p t (c i) -> p c t i", i=2),
                                    neg_tl_wu[:, :, half].rearrange("p t (c i) -> p c t i", i=2), ALU.mult)
        glq = (keep.tile([P, SLOTS], U32, name="gl_codes", align_bytes=64),
               keep.tile([P, SLOTS], U8, name="gl_scales", align_bytes=64))
        for half in halves:
            nc.vector.quantize_mx(out=glq[0][:, half].bitcast(E5M2), scales=glq[1][:, half],
                                  in_=gl[:, half, :].rearrange("p i t -> p (i t)"))
        po_q_rest = keep.tile([P, PACK - 1, SLOTS], F32, name="po_q_rest", tag="gl", align_bytes=64)
        for t in range(1, PACK):
            po_times_q(po_q_rest[:, t - 1, :], t)
        po_q = [po_q_first[:]] + [po_q_rest[:, n, :] for n in range(PACK - 1)]

        def gradient_tile(window, grad, acc, j, out):
            product(acc, xq_r, j, grad, E5M2)
            staged = stage.tile([P, SLOTS], F32, name="staged")
            nc.scalar.copy(staged[:], flat(acc))
            nc.vector.tensor_copy(window[:].indirect(offsets[:]), staged[:])
            nc.sync.dma_start(out=out.rearrange("(p j) c -> j p c", j=PACK)[j], in_=window[:])

        def window_of(tile_number):
            return windows[tile_number % len(windows)]

        for j in range(PACK // 2):
            gradient_tile(window_of(j), glq, bank_a("d1_%d" % j), j, out_0)
        gm_t = keep.tile([P, PACK, 2, P, 2], BF16, name="gm_t")
        for k in range(PACK):
            turned = bank_b("gm_turned%d" % k)
            for t in range(PACK):
                nc.tensor.transpose(turned[:, t, :], po_q[t][:, k * P:(k + 1) * P], ident[:])
            nc.scalar.activation(gm_t[:, k, :, :, :], turned[:].rearrange("n (u h) s -> n u s h", h=2), ACT.Copy,
                                 scale=tm_col[:, k:k + 1])
        for j in range(PACK // 2, PACK):
            gradient_tile(window_of(j), glq, bank_a("d1_%d" % j), j, out_0)
        gm_t_words = gm_t[:].rearrange("n k u s h -> n (k u s h)").bitcast(F32)
        gm = keep.tile([P, SLOTS, PACK], BF16, name="gm", align_bytes=64)
        gm_words = flat(gm).bitcast(F32).rearrange("s (k n u) -> s k n u", k=PACK, u=2)
        for k0 in range(0, PACK, 2):
            back = bank_b("gm_back%d" % (k0 // 2))
            for block in range(PACK):
                first = (2 * k0 + block) * P
                nc.tensor.transpose(back[:, block, :], gm_t_words[:, first:first + P], ident[:])
            nc.scalar.copy(gm_words[:, k0:k0 + 2, :, :], back[:].rearrange("s (k u) n -> s k n u", u=2))
        gmq = quantise("gm", flat(gm), E5M2)

        for j in range(PACK):
            gradient_tile(window_of(PACK + j), gmq, bank_b("d2_%d" % j), j, out_1)
